import numpy as np
import ml_dtypes

BF16 = ml_dtypes.bfloat16


def bf(x):
    return np.asarray(x, np.float32).astype(BF16)


def f32(x):
    return np.asarray(x, np.float32)


def f64(x):
    return np.asarray(x).astype(np.float64)


def striped(idx):
    return np.tile(idx.reshape(-1, 16).T, (8, 1))


S, K, M, N, D, V = 1024, 256, 128, 512, 4, 128


def setup_inputs():
    return {"table": bf(np.random.standard_normal((K, S))), "w": bf(np.random.standard_normal((D, K, M)) / np.sqrt(D * K)), "b": f32(0.5 * np.random.standard_normal((M, 1))), "offs": striped(np.random.permutation(S)[:N])}


def reference(table, w, b, offs):
    idx = offs[:16].T.reshape(-1)
    x = f64(table)[:, idx]
    y = sum(f64(w)[t].T @ x[:, t * V : (t + 1) * V] for t in range(D))
    return np.tanh(y + f64(b))

@@ -1,0 +1,54 @@
+import concourse.mybir as mybir
+
+BF16, F32, U16 = mybir.dt.bfloat16, mybir.dt.float32, mybir.dt.uint16
+TANH = mybir.ActivationFunctionType.Tanh
+
+P = 128
+PER_COLUMN = 16
+
+FLOPS = 2 * 4 * 256 * 128 * 128
+
+
+def tile_gather_matmul_kernel(tc, table, w, b, offs, out):
+    nc = tc.nc
+    n_features, n_nodes = table.shape
+    n_relations, _, n_out = w.shape
+    n_picked = out.shape[1]
+    n_blocks = n_features // P
+    piece = n_picked // PER_COLUMN
+
+    with (
+        tc.tile_pool(name="held", bufs=1) as held,
+        tc.psum_pool(name="psum", bufs=1) as psum,
+    ):
+        offsets = held.tile([P, offs.shape[1]], U16, name="offsets")
+        nc.sync.dma_start(offsets[:], offs)
+
+        table_blocks = []
+        weight_blocks = []
+        for a in range(n_blocks):
+            rows = slice(a * P, (a + 1) * P)
+            table_block = held.tile([P, n_nodes], BF16, name="table_block%d" % a)
+            nc.sync.dma_start(table_block[:], table[rows, :])
+            table_blocks.append(table_block)
+            weight_block = held.tile([P, n_relations, n_out], BF16, name="weight_block%d" % a)
+            nc.scalar.dma_start(weight_block[:], w[:, rows, :].rearrange("t p m -> p t m"))
+            weight_blocks.append(weight_block)
+
+        bias = held.tile([P, 1], F32, name="bias")
+        nc.scalar.dma_start(bias[:], b)
+
+        y = psum.tile([n_out, n_picked], F32, name="y")
+        steps = [(a, t) for a in range(n_blocks) for t in range(n_relations)]
+        for a, t in steps:
+            nc.tensor.matmul(
+                y[:],
+                weight_blocks[a][:, t, :],
+                table_blocks[a][:].indirect(offsets[:, t * piece : (t + 1) * piece]),
+                start=(a, t) == steps[0],
+                stop=(a, t) == steps[-1],
+            )
+
+        result = held.tile([n_out, n_picked], F32, name="result")
+        nc.scalar.activation(result[:], y[:], TANH, bias=bias[:])
+        nc.sync.dma_start(out, result[:])

@@ -5,14 +5,17 @@ TANH = mybir.ActivationFunctionType.Tanh
 
 P = 128
 PER_COLUMN = 16
+BANK = 512
 
 FLOPS = 2 * 4 * 256 * 128 * 128
+
+N_IDLE = 12
 
 
 def tile_gather_matmul_kernel(tc, table, w, b, offs, out):
     nc = tc.nc
     n_features, n_nodes = table.shape
-    n_relations, _, n_out = w.shape
+    n_relations, n_out = w.shape[0], w.shape[2]
     n_picked = out.shape[1]
     n_blocks = n_features // P
     piece = n_picked // PER_COLUMN
@@ -21,22 +24,34 @@ def tile_gather_matmul_kernel(tc, table, w, b, offs, out):
         tc.tile_pool(name="held", bufs=1) as held,
         tc.psum_pool(name="psum", bufs=1) as psum,
     ):
+        idle_zeros = held.tile([P, P], BF16, name="idle_zeros")
+        nc.vector.memset(idle_zeros[:], 0.0)
+        idle_scalar = held.tile([P, 1], F32, name="idle_scalar")
+        nc.vector.memset(idle_scalar[:], 0.0)
+
         offsets = held.tile([P, offs.shape[1]], U16, name="offsets")
         nc.sync.dma_start(offsets[:], offs)
 
-        table_blocks = []
-        weight_blocks = []
-        for a in range(n_blocks):
-            rows = slice(a * P, (a + 1) * P)
-            table_block = held.tile([P, n_nodes], BF16, name="table_block%d" % a)
-            nc.sync.dma_start(table_block[:], table[rows, :])
-            table_blocks.append(table_block)
-            weight_block = held.tile([P, n_relations, n_out], BF16, name="weight_block%d" % a)
-            nc.scalar.dma_start(weight_block[:], w[:, rows, :].rearrange("t p m -> p t m"))
-            weight_blocks.append(weight_block)
-
+        table_blocks = [held.tile([P, n_nodes], BF16, name="table_block%d" % a) for a in range(n_blocks)]
+        weight_blocks = [held.tile([P, n_relations, n_out], BF16, name="weight_block%d" % a) for a in range(n_blocks)]
         bias = held.tile([P, 1], F32, name="bias")
+
+        def load_table(queue, a):
+            queue.dma_start(table_blocks[a][:], table[a * P : (a + 1) * P, :])
+
+        def load_weights(queue, a):
+            queue.dma_start(weight_blocks[a][:], w[:, a * P : (a + 1) * P, :].rearrange("t p m -> p t m"))
+
+        load_table(nc.sync, 0)
+        load_weights(nc.scalar, 0)
+        load_table(nc.sync, 1)
+        load_weights(nc.scalar, 1)
         nc.scalar.dma_start(bias[:], b)
+
+        nc.scalar.activation(idle_scalar[:], idle_scalar[:], TANH)
+        idle_bank = psum.tile([P, P], F32, name="idle_bank")
+        for i in range(N_IDLE):
+            nc.tensor.matmul(idle_bank[:], idle_zeros[:], idle_zeros[:], start=True, stop=True)
 
         y = psum.tile([n_out, n_picked], F32, name="y")
         steps = [(a, t) for a in range(n_blocks) for t in range(n_relations)]

@@ -33,19 +33,13 @@ def tile_gather_matmul_kernel(tc, table, w, b, offs, out):
         nc.sync.dma_start(offsets[:], offs)
 
         table_blocks = [held.tile([P, n_nodes], BF16, name="table_block%d" % a) for a in range(n_blocks)]
-        weight_blocks = [held.tile([P, n_relations, n_out], BF16, name="weight_block%d" % a) for a in range(n_blocks)]
+        weights = held.tile([P, n_relations, n_blocks, n_out], BF16, name="weights")
         bias = held.tile([P, 1], F32, name="bias")
 
-        def load_table(queue, a):
-            queue.dma_start(table_blocks[a][:], table[a * P : (a + 1) * P, :])
-
-        def load_weights(queue, a):
-            queue.dma_start(weight_blocks[a][:], w[:, a * P : (a + 1) * P, :].rearrange("t p m -> p t m"))
-
-        load_table(nc.sync, 0)
-        load_weights(nc.scalar, 0)
-        load_table(nc.sync, 1)
-        load_weights(nc.scalar, 1)
+        table_by_block = table.rearrange("(p a) s -> p a s", a=n_blocks)
+        nc.scalar.dma_start(weights[:], w.rearrange("t (p a) m -> p t a m", a=n_blocks))
+        for a in range(n_blocks):
+            nc.sync.dma_start(table_blocks[a][:], table_by_block[:, a, :])
         nc.scalar.dma_start(bias[:], b)
 
         nc.scalar.activation(idle_scalar[:], idle_scalar[:], TANH)
@@ -58,7 +52,7 @@ def tile_gather_matmul_kernel(tc, table, w, b, offs, out):
         for a, t in steps:
             nc.tensor.matmul(
                 y[:],
-                weight_blocks[a][:, t, :],
+                weights[:, t, a, :],
                 table_blocks[a][:].indirect(offsets[:, t * piece : (t + 1) * piece]),
                 start=(a, t) == steps[0],
                 stop=(a, t) == steps[-1],

@@ -5,11 +5,8 @@ TANH = mybir.ActivationFunctionType.Tanh
 
 P = 128
 PER_COLUMN = 16
-BANK = 512
 
 FLOPS = 2 * 4 * 256 * 128 * 128
-
-N_IDLE = 12
 
 
 def tile_gather_matmul_kernel(tc, table, w, b, offs, out):
@@ -24,8 +21,6 @@ def tile_gather_matmul_kernel(tc, table, w, b, offs, out):
         tc.tile_pool(name="held", bufs=1) as held,
         tc.psum_pool(name="psum", bufs=1) as psum,
     ):
-        idle_zeros = held.tile([P, P], BF16, name="idle_zeros")
-        nc.vector.memset(idle_zeros[:], 0.0)
         idle_scalar = held.tile([P, 1], F32, name="idle_scalar")
         nc.vector.memset(idle_scalar[:], 0.0)
 
@@ -43,9 +38,6 @@ def tile_gather_matmul_kernel(tc, table, w, b, offs, out):
         nc.scalar.dma_start(bias[:], b)
 
         nc.scalar.activation(idle_scalar[:], idle_scalar[:], TANH)
-        idle_bank = psum.tile([P, P], F32, name="idle_bank")
-        for i in range(N_IDLE):
-            nc.tensor.matmul(idle_bank[:], idle_zeros[:], idle_zeros[:], start=True, stop=True)
 
         y = psum.tile([n_out, n_picked], F32, name="y")
         steps = [(a, t) for a in range(n_blocks) for t in range(n_relations)]

@@ -5,6 +5,7 @@ TANH = mybir.ActivationFunctionType.Tanh
 
 P = 128
 PER_COLUMN = 16
+ROW_START = 256
 
 FLOPS = 2 * 4 * 256 * 128 * 128
 
@@ -27,8 +28,10 @@ def tile_gather_matmul_kernel(tc, table, w, b, offs, out):
         offsets = held.tile([P, offs.shape[1]], U16, name="offsets")
         nc.sync.dma_start(offsets[:], offs)
 
-        table_blocks = [held.tile([P, n_nodes], BF16, name="table_block%d" % a) for a in range(n_blocks)]
-        weights = held.tile([P, n_relations, n_blocks, n_out], BF16, name="weights")
+        table_blocks = [
+            held.tile([P, n_nodes], BF16, name="table_block%d" % a, align_bytes=ROW_START) for a in range(n_blocks)
+        ]
+        weights = held.tile([P, n_relations, n_blocks, n_out], BF16, name="weights", align_bytes=ROW_START)
         bias = held.tile([P, 1], F32, name="bias")
 
         table_by_block = table.rearrange("(p a) s -> p a s", a=n_blocks)
@@ -50,6 +53,6 @@ def tile_gather_matmul_kernel(tc, table, w, b, offs, out):
                 stop=(a, t) == steps[-1],
             )
 
-        result = held.tile([n_out, n_picked], F32, name="result")
+        result = held.tile([n_out, n_picked], F32, name="result", align_bytes=ROW_START)
         nc.scalar.activation(result[:], y[:], TANH, bias=bias[:])
         nc.sync.dma_start(out, result[:])

@@ -7,6 +7,8 @@ P = 128
 PER_COLUMN = 16
 ROW_START = 256
 
+N_IDLE = 2048 // P
+
 FLOPS = 2 * 4 * 256 * 128 * 128
 
 
@@ -22,6 +24,8 @@ def tile_gather_matmul_kernel(tc, table, w, b, offs, out):
         tc.tile_pool(name="held", bufs=1) as held,
         tc.psum_pool(name="psum", bufs=1) as psum,
     ):
+        idle_zeros = held.tile([P, P], BF16, name="idle_zeros")
+        nc.vector.memset(idle_zeros[:], 0.0)
         idle_scalar = held.tile([P, 1], F32, name="idle_scalar")
         nc.vector.memset(idle_scalar[:], 0.0)
 
@@ -41,6 +45,9 @@ def tile_gather_matmul_kernel(tc, table, w, b, offs, out):
         nc.scalar.dma_start(bias[:], b)
 
         nc.scalar.activation(idle_scalar[:], idle_scalar[:], TANH)
+        idle_bank = psum.tile([P, P], F32, name="idle_bank")
+        for i in range(N_IDLE):
+            nc.tensor.matmul(idle_bank[:], idle_zeros[:], idle_zeros[:], start=True, stop=True)
 
         y = psum.tile([n_out, n_picked], F32, name="y")
         steps = [(a, t) for a in range(n_blocks) for t in range(n_relations)]

@@ -30,7 +30,6 @@ def tile_gather_matmul_kernel(tc, table, w, b, offs, out):
         nc.vector.memset(idle_scalar[:], 0.0)
 
         offsets = held.tile([P, offs.shape[1]], U16, name="offsets")
-        nc.sync.dma_start(offsets[:], offs)
 
         table_blocks = [
             held.tile([P, n_nodes], BF16, name="table_block%d" % a, align_bytes=ROW_START) for a in range(n_blocks)
@@ -40,7 +39,9 @@ def tile_gather_matmul_kernel(tc, table, w, b, offs, out):
 
         table_by_block = table.rearrange("(p a) s -> p a s", a=n_blocks)
         nc.scalar.dma_start(weights[:], w.rearrange("t (p a) m -> p t a m", a=n_blocks))
-        for a in range(n_blocks):
+        nc.sync.dma_start(table_blocks[0][:], table_by_block[:, 0, :])
+        nc.sync.dma_start(offsets[:], offs)
+        for a in range(1, n_blocks):
             nc.sync.dma_start(table_blocks[a][:], table_by_block[:, a, :])
         nc.scalar.dma_start(bias[:], b)
 

import concourse.mybir as mybir

BF16, F32, U16 = mybir.dt.bfloat16, mybir.dt.float32, mybir.dt.uint16
TANH = mybir.ActivationFunctionType.Tanh

P = 128
PER_COLUMN = 16
ROW_START = 256

N_IDLE = 2048 // P

FLOPS = 2 * 4 * 256 * 128 * 128


def tile_gather_matmul_kernel(tc, table, w, b, offs, out):
    nc = tc.nc
    n_features, n_nodes = table.shape
    n_relations, n_out = w.shape[0], w.shape[2]
    n_picked = out.shape[1]
    n_blocks = n_features // P
    piece = n_picked // PER_COLUMN

    with (
        tc.tile_pool(name="held", bufs=1) as held,
        tc.psum_pool(name="psum", bufs=1) as psum,
    ):
        idle_zeros = held.tile([P, P], BF16, name="idle_zeros")
        nc.vector.memset(idle_zeros[:], 0.0)
        idle_scalar = held.tile([P, 1], F32, name="idle_scalar")
        nc.vector.memset(idle_scalar[:], 0.0)

        offsets = held.tile([P, offs.shape[1]], U16, name="offsets")

        table_blocks = [
            held.tile([P, n_nodes], BF16, name="table_block%d" % a, align_bytes=ROW_START) for a in range(n_blocks)
        ]
        weights = held.tile([P, n_relations, n_blocks, n_out], BF16, name="weights", align_bytes=ROW_START)
        bias = held.tile([P, 1], F32, name="bias")

        table_by_block = table.rearrange("(p a) s -> p a s", a=n_blocks)
        nc.scalar.dma_start(weights[:], w.rearrange("t (p a) m -> p t a m", a=n_blocks))
        nc.sync.dma_start(table_blocks[0][:], table_by_block[:, 0, :])
        nc.sync.dma_start(offsets[:], offs)
        for a in range(1, n_blocks):
            nc.sync.dma_start(table_blocks[a][:], table_by_block[:, a, :])
        nc.scalar.dma_start(bias[:], b)

        nc.scalar.activation(idle_scalar[:], idle_scalar[:], TANH)
        idle_bank = psum.tile([P, P], F32, name="idle_bank")
        for i in range(N_IDLE):
            nc.tensor.matmul(idle_bank[:], idle_zeros[:], idle_zeros[:], start=True, stop=True)

        y = psum.tile([n_out, n_picked], F32, name="y")
        steps = [(a, t) for a in range(n_blocks) for t in range(n_relations)]
        for a, t in steps:
            nc.tensor.matmul(
                y[:],
                weights[:, t, a, :],
                table_blocks[a][:].indirect(offsets[:, t * piece : (t + 1) * piece]),
                start=(a, t) == steps[0],
                stop=(a, t) == steps[-1],
            )

        result = held.tile([n_out, n_picked], F32, name="result", align_bytes=ROW_START)
        nc.scalar.activation(result[:], y[:], TANH, bias=bias[:])
        nc.sync.dma_start(out, result[:])
